import numpy as np
import ml_dtypes


def mxq(x, axis, fmt="e4m3"):
    dtype, down = {"e4m3": (ml_dtypes.float8_e4m3fn, 7), "e5m2": (ml_dtypes.float8_e5m2, 14)}[fmt]
    v = np.moveaxis(np.asarray(x, np.float32).astype(ml_dtypes.bfloat16).astype(np.float64), axis, -1)
    blocks = v.reshape(v.shape[:-1] + (-1, 32))
    amax = np.abs(blocks).max(-1, keepdims=True)
    byte = np.maximum(np.where(amax > 0, np.frexp(amax)[1] - 1 + 127, 0) - down, 1)
    scale = np.exp2(byte - 127.0)
    codes = (blocks / scale).astype(np.float32).astype(dtype).astype(np.float64)
    return np.moveaxis((codes * scale).reshape(v.shape), -1, axis)


WIDE = False


def mx_kscale(k):
    if not WIDE:
        return np.ones(k)
    levels = np.array([10, -10, 5, -5, 0])
    if k % 512:
        return np.exp2(np.random.permutation(np.resize(levels, k // 32))).repeat(32)
    a = np.empty((k // 512, 16))
    for p in range(k // 512):
        a[p, :8] = np.random.permutation(np.resize(levels, 8))
        for g in range(8):
            far = levels[np.abs(levels - a[p, g]) >= 10]
            a[p, g + 8] = far[np.random.randint(len(far))]
    return np.exp2(a.ravel()).repeat(32)


def f64(x):
    return np.asarray(x).astype(np.float64)


def striped(idx):
    return np.tile(np.asarray(idx).reshape(-1, 16).T, (8, 1)).astype(np.uint16)


def unstriped(offs):
    return offs[:16].T.reshape(-1).astype(np.int64)


E2M1 = np.array([0.0, 0.5, 1.0, 1.5, 2.0, 3.0, 4.0, 6.0, -0.0, -0.5, -1.0, -1.5, -2.0, -3.0, -4.0, -6.0])


def pack_weight(w, fmt):
    k, n = w.shape
    w = f64(np.asarray(w, np.float32).astype(ml_dtypes.bfloat16)).reshape(k // 32, 32, n)
    amax = np.abs(w).max(1)
    if fmt == "e4m3":
        byte = np.frexp(amax)[1] - 1 + 127 - 7
    else:
        mant, ex = np.frexp(amax / 6.0)
        byte = np.where(mant > 0.5, ex, ex - 1) + 127
    byte = np.clip(np.where(amax > 0, byte, 1), 1, 254)
    scaled = (w * np.exp2(127.0 - byte)[:, None, :]).reshape(k, n).astype(np.float32)
    by_word = np.ascontiguousarray(scaled.reshape(k // 512, 128, 4, n).transpose(0, 1, 3, 2))
    if fmt == "e4m3":
        words = by_word.astype(ml_dtypes.float8_e4m3fn).view(np.uint8)
    else:
        c = by_word.astype(ml_dtypes.float4_e2m1fn).view(np.uint8) & 0xF
        words = (c[..., 0::2] | (c[..., 1::2] << 4)).reshape(k // 512, 128, 2 * n)
    return np.ascontiguousarray(words), np.ascontiguousarray(byte.astype(np.uint8).reshape(k // 512, 16, n))


def unpack_weight(words, scales, fmt):
    g, _, n = scales.shape
    words = np.ascontiguousarray(words).reshape(g, 128, n, -1)
    if fmt == "e4m3":
        vals = words.view(ml_dtypes.float8_e4m3fn).astype(np.float64)
    else:
        nib = np.empty((g, 128, n, 4), np.uint8)
        nib[..., 0::2] = words & 0xF
        nib[..., 1::2] = words >> 4
        vals = E2M1[nib]
    vals = vals * np.repeat(np.exp2(scales.astype(np.float64) - 127.0), 8, axis=1)[..., None]
    return vals.transpose(0, 1, 3, 2).reshape(g * 512, n)


def softplus(v):
    return np.log(1.0 + np.exp(v))


D, K, R, T, I, Q = 512, 512, 512, 2048, 512, 128


def setup_inputs():
    n = np.random.standard_normal
    idx3 = np.random.permutation(I)[:I]
    idx = np.random.permutation(T)[:I]
    fd = mx_kscale(D)
    fk = mx_kscale(K)
    fr = mx_kscale(R)
    keysp = pack_weight(n((D, T)) / fd[:, None], "e4m3")
    tabp = pack_weight(n((K, T)) / fk[:, None], "e4m3")
    return {
        "query": (n((D, Q)) * 0.7 / np.sqrt(D) * fd[:, None]).astype(np.float32),
        "keys_words": keysp[0],
        "keys_scales": keysp[1],
        "tab_words": tabp[0],
        "tab_scales": tabp[1],
        "w1": (n((K, R)) * 1 / np.sqrt(K) * fk[:, None]).astype(np.float32),
        "lam": (np.random.uniform(0.3, 1.0, (R, 1))).astype(np.float32),
        "gout": (n((R, Q)) * 1 / np.sqrt(R) * fr[:, None]).astype(np.float32),
        "hsc": (np.random.uniform(0.7, 1.4, (R, 1)) / fr[:, None]).astype(np.float32),
        "old": (0.5 * n((Q, T))).astype(np.float32),
        "offs3": striped(idx3),
        "offs": striped(idx),
    }


def reference(query, keys_words, keys_scales, tab_words, tab_scales, w1, lam, gout, hsc, old, offs3, offs):
    idx3 = unstriped(offs3)
    idx = unstriped(offs)
    keysu = unpack_weight(keys_words, keys_scales, "e4m3")
    tabu = unpack_weight(tab_words, tab_scales, "e4m3")
    queryq = mxq(f64(query), 0, "e4m3")
    keysidxg = keysu[:, idx]
    a = queryq.T @ keysidxg
    p = np.exp(a - np.max(a, axis=1, keepdims=True))
    z = np.sum(p, axis=1, keepdims=True)
    w1q = mxq(f64(w1), 0, "e4m3")
    tabidxg = tabu[:, idx]
    zh = w1q.T @ tabidxg
    ht = softplus(zh)
    hv = ht + ht[:, idx3] * f64(lam)
    hs1 = hv * f64(hsc)
    goutq = mxq(f64(gout), 0, "e4m3")
    hs1q = mxq(hs1, 0, "e4m3")
    c0 = goutq.T @ hs1q
    dz = np.sum(c0 * p / np.square(z) * (-1.0), axis=1, keepdims=True)
    dp = c0 / z + dz
    da = dp * p
    gs = da * 512.0
    gf = np.zeros((Q, T))
    gf[:, idx] = gs
    y = f64(old) + gf
    return y

@@ -1,0 +1,217 @@
+from contextlib import ExitStack
+
+import concourse.mybir as mybir
+
+F32 = mybir.dt.float32
+BF16 = mybir.dt.bfloat16
+I32 = mybir.dt.int32
+U32 = mybir.dt.uint32
+U16 = mybir.dt.uint16
+U8 = mybir.dt.uint8
+FP8X4 = mybir.dt.float8_e4m3fn_x4
+ALU = mybir.AluOpType
+ACT = mybir.ActivationFunctionType
+AXIS_X = mybir.AxisListType.X
+
+P = 128
+PACK = 4
+POOL = 2048
+SLOTS = 512
+HIDDEN = 512
+ROWS = 128
+HALF = SLOTS // 2
+GRAD_SCALE = 512.0
+EXP_CAP = 2.0**56
+W1_SCALAR_COLS = 56
+OUT_CHUNKS = (512, 512, 512, 512)
+
+AT_W1 = 0
+AT_TAB = 12288
+
+FLOPS = 2 * 512 * SLOTS * (ROWS + HIDDEN + ROWS)
+
+
+def tile_attend_blrlent_soft_kernel(
+    tc, query, keys_words, keys_scales, tab_words, tab_scales, w1, lam, gout, hsc, old, offs3, offs, out
+):
+    nc = tc.nc
+    with ExitStack() as ctx:
+        held = ctx.enter_context(tc.tile_pool(name="held", bufs=1))
+        early = ctx.enter_context(tc.tile_pool(name="early", bufs=1))
+        psum = ctx.enter_context(tc.psum_pool(name="psum", bufs=1))
+
+        def sbuf(name, shape, dtype, tag=None):
+            return held.tile(shape, dtype, name=name, tag=tag or name, align_bytes=64)
+
+        def reused(name, shape, dtype, offset):
+            return early.tile(shape, dtype, name=name, offset=offset, align_bytes=64)
+
+        def load_words(tile, words):
+            nc.sync.dma_start(out=tile[:].bitcast(I32), in_=words[0].rearrange("p n t -> p (n t)").bitcast(I32))
+            return tile
+
+        def load_scales(tile, scales, clearing, queue):
+            clearing.memset(tile[:].bitcast(I32), 0)
+            for quad in range(4):
+                queue.dma_start(
+                    out=tile[32 * quad : 32 * quad + 4, :].bitcast(I32),
+                    in_=scales[0, 4 * quad : 4 * quad + 4, :].bitcast(I32),
+                )
+            return tile
+
+        def load_rows(tile, rows, queue):
+            queue.dma_start(out=tile[:], in_=rows.rearrange("(p j) c -> p j c", j=PACK))
+            return tile
+
+        def gather(tile, window, offsets):
+            nc.vector.tensor_copy(out=tile[:], in_=window[:].indirect(offsets[:]))
+            return tile
+
+        def interleave(tile, planes):
+            nc.vector.tensor_copy(
+                out=tile[:].rearrange("p (c i) j -> p c j i", i=4),
+                in_=planes.rearrange("p j (c i) -> p c j i", i=4),
+            )
+            return tile
+
+        def quantize(name, grouped, width):
+            codes = sbuf(name + "_codes", [P, width], U32)
+            plane = sbuf(name + "_plane", [P, width], U8)
+            nc.vector.quantize_mx(out=codes[:].bitcast(FP8X4), scales=plane[:], in_=grouped)
+            return codes, plane
+
+        def product(bank, lhs_codes, lhs_plane, rhs_codes, rhs_plane):
+            nc.tensor.matmul_mx(
+                out=bank,
+                lhsT=lhs_codes.bitcast(FP8X4),
+                lhsT_scale=lhs_plane,
+                rhs=rhs_codes.bitcast(FP8X4),
+                rhs_scale=rhs_plane,
+                start=True,
+                stop=True,
+            )
+
+        token_list = held.tile([P, SLOTS // 16], U16, name="token_list")
+        nc.sync.dma_start(token_list[:], offs)
+        w1_rows = load_rows(reused("w1_rows", [P, PACK, HIDDEN], F32, AT_W1), w1, nc.sync)
+        tab_pool = load_words(reused("tab_pool", [P, POOL], U32, AT_TAB), tab_words)
+        tab_bytes = sbuf("tab_bytes", [P, POOL], U8)
+        load_scales(tab_bytes, tab_scales, nc.gpsimd, nc.scalar)
+        link_list = held.tile([P, SLOTS // 16], U16, name="link_list")
+        nc.sync.dma_start(link_list[:], offs3)
+
+        placed = sbuf("placed", [P, POOL], F32)
+        nc.gpsimd.memset(placed[:], 0.0)
+
+        tab_plane = gather(sbuf("tab_plane", [P, SLOTS], U8), tab_bytes, token_list)
+        w1_grouped = sbuf("w1_grouped", [P, PACK, P, PACK], BF16)
+        w1_dealt = w1_grouped[:].rearrange("p t m j -> p m j t")
+        w1_source = w1_rows[:].rearrange("p j (m t) -> p m j t", t=PACK)
+        nc.scalar.activation(out=w1_dealt[:, :W1_SCALAR_COLS], in_=w1_source[:, :W1_SCALAR_COLS], func=ACT.Copy)
+        nc.vector.tensor_copy(out=w1_dealt[:, W1_SCALAR_COLS:], in_=w1_source[:, W1_SCALAR_COLS:])
+        query_rows = load_rows(reused("query_rows", [P, PACK, ROWS], F32, AT_W1 + 2048), query, nc.sync)
+        keys_pool = load_words(reused("keys_pool", [P, POOL], U32, AT_W1 + 4096), keys_words)
+        keys_bytes = load_scales(reused("keys_bytes", [P, POOL], U8, AT_W1), keys_scales, nc.gpsimd, nc.scalar)
+        w1_codes, w1_plane = quantize("w1", w1_grouped[:].rearrange("p t m j -> p (t m j)"), HIDDEN)
+        tab_codes = gather(sbuf("tab_codes", [P, SLOTS], U32), tab_pool, token_list)
+        lam_rows = load_rows(reused("lam_rows", [P, PACK, 1], F32, AT_TAB), lam, nc.sync)
+        hsc_rows = load_rows(reused("hsc_rows", [P, PACK, 1], F32, AT_TAB + 64), hsc, nc.sync)
+        gout_rows = load_rows(reused("gout_rows", [P, PACK, ROWS], F32, AT_TAB + 128), gout, nc.sync)
+        old_rows = reused("old_rows", [P, POOL], F32, AT_TAB + 4096)
+        nc.sync.dma_start(out=old_rows[:], in_=old)
+
+        zh = [psum.tile([P, SLOTS], F32, name="zh%d" % t) for t in range(PACK)]
+        grown = [sbuf("grown%d" % t, [P, SLOTS], F32) for t in range(PACK)]
+        for t in range(PACK):
+            cols = slice(P * t, P * (t + 1))
+            product(zh[t][:], w1_codes[:, cols], w1_plane[:, cols], tab_codes[:], tab_plane[:])
+            nc.scalar.activation(out=grown[t][:], in_=zh[t][:], func=ACT.Exp)
+
+        for t in range(PACK):
+            nc.vector.tensor_scalar(
+                out=grown[t][:], in0=grown[t][:], scalar1=EXP_CAP, scalar2=1.0, op0=ALU.min, op1=ALU.add
+            )
+
+        query_grouped = interleave(reused("query_grouped", [P, ROWS, PACK], BF16, AT_TAB + 2304), query_rows[:])
+        keys_plane = gather(sbuf("keys_plane", [P, SLOTS], U8), keys_bytes, token_list)
+        query_codes, query_plane = quantize("query", query_grouped[:].rearrange("p c j -> p (c j)"), ROWS)
+        keys_codes = gather(sbuf("keys_codes", [P, SLOTS], U32), keys_pool, token_list)
+        scores = psum.tile([P, SLOTS], F32, name="scores")
+        product(scores[:], query_codes[:], query_plane[:], keys_codes[:], keys_plane[:])
+        neg_max = sbuf("neg_max", [P, 1], F32)
+        nc.vector.tensor_reduce(out=neg_max[:], in_=scores[:], axis=AXIS_X, op=ALU.max, negate=True)
+
+        gout_grouped = interleave(sbuf("gout_grouped", [P, ROWS, PACK], BF16), gout_rows[:])
+        lam_hsc = sbuf("lam_hsc", [P, PACK], F32)
+        nc.vector.tensor_tensor(out=lam_hsc[:], in0=lam_rows[:, :, 0], in1=hsc_rows[:, :, 0], op=ALU.mult)
+        gout_codes, gout_plane = quantize("gout", gout_grouped[:].rearrange("p c j -> p (c j)"), ROWS)
+
+        ht = []
+        own = []
+        for t in range(PACK):
+            logs = sbuf("logs%d" % t, [P, SLOTS], F32)
+            nc.scalar.activation(out=logs[:], in_=grown[t][:], func=ACT.Ln)
+            ht.append(sbuf("ht%d" % t, [P, SLOTS], F32))
+            nc.vector.tensor_tensor(out=ht[t][:], in0=logs[:], in1=zh[t][:], op=ALU.max)
+        for t in range(PACK):
+            own.append(sbuf("own%d" % t, [P, SLOTS], F32))
+            nc.vector.tensor_scalar(
+                out=own[t][:], in0=ht[t][:], scalar1=hsc_rows[:, t, :], scalar2=None, op0=ALU.mult
+            )
+
+        linked = {}
+        for h, t in [(1, 2), (1, 3)] + [(0, t) for t in range(PACK)] + [(1, 0), (1, 1)]:
+            links = link_list[:, HALF // 16 * h : HALF // 16 * (h + 1)]
+            linked[h, t] = sbuf("linked%d_%d" % (t, h), [P, HALF], F32)
+            if h == 1 and t >= 2:
+                nc.vector.tensor_copy(out=linked[h, t][:], in_=ht[t][:].indirect(links))
+            else:
+                nc.scalar.activation(out=linked[h, t][:], in_=ht[t][:].indirect(links), func=ACT.Copy)
+
+        p = sbuf("p", [P, SLOTS], F32, tag="ht1")
+        z = sbuf("z", [P, 1], F32)
+        nc.scalar.activation(out=p[:], in_=scores[:], func=ACT.Exp, bias=neg_max[:], accum_out=z[:])
+
+        c0 = psum.tile([P, SLOTS], F32, name="c0")
+        for h in range(2):
+            cols = slice(HALF * h, HALF * (h + 1))
+            hs1 = sbuf("hs1_%d" % h, [P, PACK, HALF], BF16)
+            for t in range(PACK) if h == 0 else (2, 3, 0, 1):
+                nc.vector.scalar_tensor_tensor(
+                    out=hs1[:, t, :],
+                    in0=linked[h, t][:],
+                    scalar=lam_hsc[:, t : t + 1],
+                    in1=own[t][:, cols],
+                    op0=ALU.mult,
+                    op1=ALU.add,
+                )
+            hs1_grouped = interleave(sbuf("hs1_grouped%d" % h, [P, HALF, PACK], BF16), hs1[:])
+            hs1_codes, hs1_plane = quantize("hs1_%d" % h, hs1_grouped[:].rearrange("p c j -> p (c j)"), HALF)
+            product(c0[:, cols], gout_codes[:], gout_plane[:], hs1_codes[:], hs1_plane[:])
+
+        inv_z = sbuf("inv_z", [P, 1], F32)
+        nc.vector.reciprocal(out=inv_z[:], in_=z[:])
+        weight = sbuf("weight", [P, SLOTS], F32)
+        nc.vector.tensor_scalar(
+            out=weight[:], in0=p[:], scalar1=inv_z[:], scalar2=GRAD_SCALE, op0=ALU.mult, op1=ALU.mult
+        )
+        weighted = sbuf("weighted", [P, SLOTS], F32)
+        total = sbuf("total", [P, 1], F32)
+        nc.vector.scalar_tensor_tensor(
+            out=weighted[:], in0=c0[:], scalar=1.0, in1=weight[:], op0=ALU.mult, op1=ALU.mult, accum_out=total[:]
+        )
+        through_z = sbuf("through_z", [P, SLOTS], F32)
+        nc.vector.tensor_scalar(
+            out=through_z[:], in0=weight[:], scalar1=total[:], scalar2=-1.0 / GRAD_SCALE, op0=ALU.mult, op1=ALU.mult
+        )
+        nc.vector.tensor_tensor(
+            out=placed[:].indirect(token_list[:]), in0=weighted[:], in1=through_z[:], op=ALU.add
+        )
+
+        start = 0
+        for n, width in enumerate(OUT_CHUNKS):
+            cols = slice(start, start + width)
+            result = sbuf("result%d" % n, [P, width], F32)
+            nc.vector.tensor_tensor(out=result[:], in0=placed[:, cols], in1=old_rows[:, cols], op=ALU.add)
+            nc.sync.dma_start(out=out[:, cols], in_=result[:])
+            start = start + width

@@ -23,7 +23,7 @@ HALF = SLOTS // 2
 GRAD_SCALE = 512.0
 EXP_CAP = 2.0**56
 W1_SCALAR_COLS = 56
-OUT_CHUNKS = (512, 512, 512, 512)
+OUT_CHUNKS = (352, 352, 352, 352, 320, 320)
 
 AT_W1 = 0
 AT_TAB = 12288
@@ -74,8 +74,15 @@ def tile_attend_blrlent_soft_kernel(
             )
             return tile
 
-        def quantize(name, grouped, width):
-            codes = sbuf(name + "_codes", [P, width], U32)
+        def interleave_small(tile, planes):
+            nc.gpsimd.tensor_copy(out=tile[:], in_=planes.rearrange("p j c -> p c j"))
+            return tile
+
+        def quantize(name, grouped, width, at=None, tag=None):
+            if at is None:
+                codes = sbuf(name + "_codes", [P, width], U32, tag)
+            else:
+                codes = reused(name + "_codes", [P, width], U32, at)
             plane = sbuf(name + "_plane", [P, width], U8)
             nc.vector.quantize_mx(out=codes[:].bitcast(FP8X4), scales=plane[:], in_=grouped)
             return codes, plane
@@ -103,10 +110,14 @@ def tile_attend_blrlent_soft_kernel(
         placed = sbuf("placed", [P, POOL], F32)
         nc.gpsimd.memset(placed[:], 0.0)
 
+        constants = sbuf("constants", [P, 2], F32)
+        nc.gpsimd.memset(constants[:, 0:1], GRAD_SCALE)
+        nc.gpsimd.memset(constants[:, 1:2], -1.0)
+
         tab_plane = gather(sbuf("tab_plane", [P, SLOTS], U8), tab_bytes, token_list)
         w1_grouped = sbuf("w1_grouped", [P, PACK, P, PACK], BF16)
-        w1_dealt = w1_grouped[:].rearrange("p t m j -> p m j t")
-        w1_source = w1_rows[:].rearrange("p j (m t) -> p m j t", t=PACK)
+        w1_dealt = w1_grouped[:].rearrange("p t m j -> p m t j")
+        w1_source = w1_rows[:].rearrange("p j (m t) -> p m t j", t=PACK)
         nc.scalar.activation(out=w1_dealt[:, :W1_SCALAR_COLS], in_=w1_source[:, :W1_SCALAR_COLS], func=ACT.Copy)
         nc.vector.tensor_copy(out=w1_dealt[:, W1_SCALAR_COLS:], in_=w1_source[:, W1_SCALAR_COLS:])
         query_rows = load_rows(reused("query_rows", [P, PACK, ROWS], F32, AT_W1 + 2048), query, nc.sync)
@@ -128,47 +139,48 @@ def tile_attend_blrlent_soft_kernel(
             nc.scalar.activation(out=grown[t][:], in_=zh[t][:], func=ACT.Exp)
 
         for t in range(PACK):
-            nc.vector.tensor_scalar(
-                out=grown[t][:], in0=grown[t][:], scalar1=EXP_CAP, scalar2=1.0, op0=ALU.min, op1=ALU.add
+            nc.gpsimd.tensor_scalar(
+                out=grown[t][:], in0=grown[t][:], scalar1=EXP_CAP, scalar2=0.0, op0=ALU.min, op1=ALU.max
             )
 
-        query_grouped = interleave(reused("query_grouped", [P, ROWS, PACK], BF16, AT_TAB + 2304), query_rows[:])
-        keys_plane = gather(sbuf("keys_plane", [P, SLOTS], U8), keys_bytes, token_list)
-        query_codes, query_plane = quantize("query", query_grouped[:].rearrange("p c j -> p (c j)"), ROWS)
+        query_grouped = interleave_small(sbuf("query_grouped", [P, ROWS, PACK], BF16), query_rows[:])
+        keys_plane = gather(reused("keys_plane", [P, SLOTS], U8, AT_TAB + 3072), keys_bytes, token_list)
+        query_codes, query_plane = quantize("query", query_grouped[:].rearrange("p c j -> p (c j)"), ROWS, AT_TAB + 2304)
         keys_codes = gather(sbuf("keys_codes", [P, SLOTS], U32), keys_pool, token_list)
         scores = psum.tile([P, SLOTS], F32, name="scores")
         product(scores[:], query_codes[:], query_plane[:], keys_codes[:], keys_plane[:])
         neg_max = sbuf("neg_max", [P, 1], F32)
         nc.vector.tensor_reduce(out=neg_max[:], in_=scores[:], axis=AXIS_X, op=ALU.max, negate=True)
 
-        gout_grouped = interleave(sbuf("gout_grouped", [P, ROWS, PACK], BF16), gout_rows[:])
+        gout_grouped = interleave_small(sbuf("gout_grouped", [P, ROWS, PACK], BF16), gout_rows[:])
         lam_hsc = sbuf("lam_hsc", [P, PACK], F32)
         nc.vector.tensor_tensor(out=lam_hsc[:], in0=lam_rows[:, :, 0], in1=hsc_rows[:, :, 0], op=ALU.mult)
-        gout_codes, gout_plane = quantize("gout", gout_grouped[:].rearrange("p c j -> p (c j)"), ROWS)
 
         ht = []
         own = []
         for t in range(PACK):
             logs = sbuf("logs%d" % t, [P, SLOTS], F32)
-            nc.scalar.activation(out=logs[:], in_=grown[t][:], func=ACT.Ln)
+            nc.scalar.activation(out=logs[:], in_=grown[t][:], func=ACT.Ln, bias=1.0)
             ht.append(sbuf("ht%d" % t, [P, SLOTS], F32))
             nc.vector.tensor_tensor(out=ht[t][:], in0=logs[:], in1=zh[t][:], op=ALU.max)
+        gout_codes, gout_plane = quantize("gout", gout_grouped[:].rearrange("p c j -> p (c j)"), ROWS, tag="logs3")
         for t in range(PACK):
             own.append(sbuf("own%d" % t, [P, SLOTS], F32))
-            nc.vector.tensor_scalar(
-                out=own[t][:], in0=ht[t][:], scalar1=hsc_rows[:, t, :], scalar2=None, op0=ALU.mult
+            engine = nc.gpsimd if t < 2 else nc.vector
+            engine.tensor_scalar(
+                out=own[t][:], in0=ht[t][:], scalar1=hsc_rows[:, t, :], scalar2=0.0, op0=ALU.mult, op1=ALU.add
             )
 
         linked = {}
-        for h, t in [(1, 2), (1, 3)] + [(0, t) for t in range(PACK)] + [(1, 0), (1, 1)]:
+        for h, t in [(1, 3)] + [(0, t) for t in range(PACK)] + [(1, 0), (1, 1), (1, 2)]:
             links = link_list[:, HALF // 16 * h : HALF // 16 * (h + 1)]
             linked[h, t] = sbuf("linked%d_%d" % (t, h), [P, HALF], F32)
-            if h == 1 and t >= 2:
+            if h == 1 and t == 3:
                 nc.vector.tensor_copy(out=linked[h, t][:], in_=ht[t][:].indirect(links))
             else:
                 nc.scalar.activation(out=linked[h, t][:], in_=ht[t][:].indirect(links), func=ACT.Copy)
 
-        p = sbuf("p", [P, SLOTS], F32, tag="ht1")
+        p = sbuf("p", [P, SLOTS], F32, tag="ht2")
         z = sbuf("z", [P, 1], F32)
         nc.scalar.activation(out=p[:], in_=scores[:], func=ACT.Exp, bias=neg_max[:], accum_out=z[:])
 
@@ -176,7 +188,7 @@ def tile_attend_blrlent_soft_kernel(
         for h in range(2):
             cols = slice(HALF * h, HALF * (h + 1))
             hs1 = sbuf("hs1_%d" % h, [P, PACK, HALF], BF16)
-            for t in range(PACK) if h == 0 else (2, 3, 0, 1):
+            for t in range(PACK) if h == 0 else (3, 0, 1, 2):
                 nc.vector.scalar_tensor_tensor(
                     out=hs1[:, t, :],
                     in0=linked[h, t][:],
@@ -191,18 +203,18 @@ def tile_attend_blrlent_soft_kernel(
 
         inv_z = sbuf("inv_z", [P, 1], F32)
         nc.vector.reciprocal(out=inv_z[:], in_=z[:])
-        weight = sbuf("weight", [P, SLOTS], F32)
+        row_factors = sbuf("row_factors", [P, 2], F32)
         nc.vector.tensor_scalar(
-            out=weight[:], in0=p[:], scalar1=inv_z[:], scalar2=GRAD_SCALE, op0=ALU.mult, op1=ALU.mult
+            out=row_factors[:], in0=constants[:], scalar1=inv_z[:], scalar2=None, op0=ALU.mult
         )
         weighted = sbuf("weighted", [P, SLOTS], F32)
         total = sbuf("total", [P, 1], F32)
         nc.vector.scalar_tensor_tensor(
-            out=weighted[:], in0=c0[:], scalar=1.0, in1=weight[:], op0=ALU.mult, op1=ALU.mult, accum_out=total[:]
+            out=weighted[:], in0=c0[:], scalar=row_factors[:, 0:1], in1=p[:], op0=ALU.mult, op1=ALU.mult, accum_out=total[:]
         )
         through_z = sbuf("through_z", [P, SLOTS], F32)
         nc.vector.tensor_scalar(
-            out=through_z[:], in0=weight[:], scalar1=total[:], scalar2=-1.0 / GRAD_SCALE, op0=ALU.mult, op1=ALU.mult
+            out=through_z[:], in0=p[:], scalar1=total[:], scalar2=row_factors[:, 1:2], op0=ALU.mult, op1=ALU.mult
         )
         nc.vector.tensor_tensor(
             out=placed[:].indirect(token_list[:]), in0=weighted[:], in1=through_z[:], op=ALU.add

@@ -26,7 +26,8 @@ W1_SCALAR_COLS = 56
 OUT_CHUNKS = (352, 352, 352, 352, 320, 320)
 
 AT_W1 = 0
-AT_TAB = 12288
+AT_TAB = 12544
+AT_GROUPED = 25856
 
 FLOPS = 2 * 512 * SLOTS * (ROWS + HIDDEN + ROWS)
 
@@ -114,84 +115,95 @@ def tile_attend_blrlent_soft_kernel(
         nc.gpsimd.memset(constants[:, 0:1], GRAD_SCALE)
         nc.gpsimd.memset(constants[:, 1:2], -1.0)
 
-        tab_plane = gather(sbuf("tab_plane", [P, SLOTS], U8), tab_bytes, token_list)
-        w1_grouped = sbuf("w1_grouped", [P, PACK, P, PACK], BF16)
+        w1_grouped = reused("w1_grouped", [P, PACK, P, PACK], BF16, AT_GROUPED)
         w1_dealt = w1_grouped[:].rearrange("p t m j -> p m t j")
         w1_source = w1_rows[:].rearrange("p j (m t) -> p m t j", t=PACK)
         nc.scalar.activation(out=w1_dealt[:, :W1_SCALAR_COLS], in_=w1_source[:, :W1_SCALAR_COLS], func=ACT.Copy)
         nc.vector.tensor_copy(out=w1_dealt[:, W1_SCALAR_COLS:], in_=w1_source[:, W1_SCALAR_COLS:])
         query_rows = load_rows(reused("query_rows", [P, PACK, ROWS], F32, AT_W1 + 2048), query, nc.sync)
-        keys_pool = load_words(reused("keys_pool", [P, POOL], U32, AT_W1 + 4096), keys_words)
+        keys_pool = load_words(reused("keys_pool", [P, POOL], U32, AT_W1 + 4224), keys_words)
+        lam_rows = load_rows(reused("lam_rows", [P, PACK, 1], F32, AT_W1 + 4096), lam, nc.sync)
+        hsc_rows = load_rows(reused("hsc_rows", [P, PACK, 1], F32, AT_W1 + 4160), hsc, nc.sync)
         keys_bytes = load_scales(reused("keys_bytes", [P, POOL], U8, AT_W1), keys_scales, nc.gpsimd, nc.scalar)
         w1_codes, w1_plane = quantize("w1", w1_grouped[:].rearrange("p t m j -> p (t m j)"), HIDDEN)
-        tab_codes = gather(sbuf("tab_codes", [P, SLOTS], U32), tab_pool, token_list)
-        lam_rows = load_rows(reused("lam_rows", [P, PACK, 1], F32, AT_TAB), lam, nc.sync)
-        hsc_rows = load_rows(reused("hsc_rows", [P, PACK, 1], F32, AT_TAB + 64), hsc, nc.sync)
+        tab_plane = reused("tab_plane", [P, SLOTS], U8, AT_GROUPED)
+        tab_codes = reused("tab_codes", [P, SLOTS], U32, AT_GROUPED + SLOTS)
+        for h in range(2):
+            slots = slice(HALF * h, HALF * (h + 1))
+            tokens = token_list[:, HALF // 16 * h : HALF // 16 * (h + 1)]
+            nc.vector.tensor_copy(out=tab_plane[:, slots], in_=tab_bytes[:].indirect(tokens))
+            nc.vector.tensor_copy(out=tab_codes[:, slots], in_=tab_pool[:].indirect(tokens))
         gout_rows = load_rows(reused("gout_rows", [P, PACK, ROWS], F32, AT_TAB + 128), gout, nc.sync)
-        old_rows = reused("old_rows", [P, POOL], F32, AT_TAB + 4096)
+        old_rows = reused("old_rows", [P, POOL], F32, AT_TAB + 5120)
         nc.sync.dma_start(out=old_rows[:], in_=old)
 
-        zh = [psum.tile([P, SLOTS], F32, name="zh%d" % t) for t in range(PACK)]
-        grown = [sbuf("grown%d" % t, [P, SLOTS], F32) for t in range(PACK)]
-        for t in range(PACK):
-            cols = slice(P * t, P * (t + 1))
-            product(zh[t][:], w1_codes[:, cols], w1_plane[:, cols], tab_codes[:], tab_plane[:])
-            nc.scalar.activation(out=grown[t][:], in_=zh[t][:], func=ACT.Exp)
-
-        for t in range(PACK):
-            nc.gpsimd.tensor_scalar(
-                out=grown[t][:], in0=grown[t][:], scalar1=EXP_CAP, scalar2=0.0, op0=ALU.min, op1=ALU.max
-            )
+        zh = {}
+        grown = {}
+        for h in range(2):
+            slots = slice(HALF * h, HALF * (h + 1))
+            for pair in range(2):
+                zh[pair, h] = psum.tile([P, 2, HALF], F32, name="zh%d_%d" % (pair, h))
+                for e in range(2):
+                    cols = slice(P * (2 * pair + e), P * (2 * pair + e + 1))
+                    product(
+                        zh[pair, h][:, e, :], w1_codes[:, cols], w1_plane[:, cols], tab_codes[:, slots], tab_plane[:, slots]
+                    )
+                grown[pair, h] = sbuf("grown%d_%d" % (pair, h), [P, 2, HALF], F32)
+                nc.scalar.activation(out=grown[pair, h][:], in_=zh[pair, h][:], func=ACT.Exp)
+                nc.gpsimd.tensor_scalar(
+                    out=grown[pair, h][:], in0=grown[pair, h][:], scalar1=EXP_CAP, scalar2=0.0, op0=ALU.min, op1=ALU.max
+                )
 
         query_grouped = interleave_small(sbuf("query_grouped", [P, ROWS, PACK], BF16), query_rows[:])
-        keys_plane = gather(reused("keys_plane", [P, SLOTS], U8, AT_TAB + 3072), keys_bytes, token_list)
         query_codes, query_plane = quantize("query", query_grouped[:].rearrange("p c j -> p (c j)"), ROWS, AT_TAB + 2304)
-        keys_codes = gather(sbuf("keys_codes", [P, SLOTS], U32), keys_pool, token_list)
+        keys_codes = gather(reused("keys_codes", [P, SLOTS], U32, AT_TAB + 3072), keys_pool, token_list)
+        keys_plane = gather(reused("keys_plane", [P, SLOTS], U8, AT_W1 + 4224), keys_bytes, token_list)
         scores = psum.tile([P, SLOTS], F32, name="scores")
         product(scores[:], query_codes[:], query_plane[:], keys_codes[:], keys_plane[:])
         neg_max = sbuf("neg_max", [P, 1], F32)
         nc.vector.tensor_reduce(out=neg_max[:], in_=scores[:], axis=AXIS_X, op=ALU.max, negate=True)
 
-        gout_grouped = interleave_small(sbuf("gout_grouped", [P, ROWS, PACK], BF16), gout_rows[:])
         lam_hsc = sbuf("lam_hsc", [P, PACK], F32)
         nc.vector.tensor_tensor(out=lam_hsc[:], in0=lam_rows[:, :, 0], in1=hsc_rows[:, :, 0], op=ALU.mult)
 
-        ht = []
+        ht = sbuf("ht", [P, PACK, SLOTS], F32)
         own = []
-        for t in range(PACK):
-            logs = sbuf("logs%d" % t, [P, SLOTS], F32)
-            nc.scalar.activation(out=logs[:], in_=grown[t][:], func=ACT.Ln, bias=1.0)
-            ht.append(sbuf("ht%d" % t, [P, SLOTS], F32))
-            nc.vector.tensor_tensor(out=ht[t][:], in0=logs[:], in1=zh[t][:], op=ALU.max)
-        gout_codes, gout_plane = quantize("gout", gout_grouped[:].rearrange("p c j -> p (c j)"), ROWS, tag="logs3")
+        for pair in range(2):
+            for h in range(2):
+                logs = sbuf("logs%d_%d" % (pair, h), [P, 2, HALF], F32)
+                nc.scalar.activation(out=logs[:], in_=grown[pair, h][:], func=ACT.Ln, bias=1.0)
+                nc.vector.tensor_tensor(
+                    out=ht[:, 2 * pair : 2 * pair + 2, HALF * h : HALF * (h + 1)], in0=logs[:], in1=zh[pair, h][:], op=ALU.max
+                )
+        gout_grouped = interleave_small(sbuf("gout_grouped", [P, ROWS, PACK], BF16, tag="grown0_0"), gout_rows[:])
+        gout_codes, gout_plane = quantize("gout", gout_grouped[:].rearrange("p c j -> p (c j)"), ROWS, tag="logs1_1")
         for t in range(PACK):
             own.append(sbuf("own%d" % t, [P, SLOTS], F32))
             engine = nc.gpsimd if t < 2 else nc.vector
             engine.tensor_scalar(
-                out=own[t][:], in0=ht[t][:], scalar1=hsc_rows[:, t, :], scalar2=0.0, op0=ALU.mult, op1=ALU.add
+                out=own[t][:], in0=ht[:, t, :], scalar1=hsc_rows[:, t, :], scalar2=0.0, op0=ALU.mult, op1=ALU.add
             )
 
-        linked = {}
+        linked = [sbuf("linked%d" % h, [P, PACK, HALF], F32) for h in range(2)]
         for h, t in [(1, 3)] + [(0, t) for t in range(PACK)] + [(1, 0), (1, 1), (1, 2)]:
             links = link_list[:, HALF // 16 * h : HALF // 16 * (h + 1)]
-            linked[h, t] = sbuf("linked%d_%d" % (t, h), [P, HALF], F32)
             if h == 1 and t == 3:
-                nc.vector.tensor_copy(out=linked[h, t][:], in_=ht[t][:].indirect(links))
+                nc.vector.tensor_copy(out=linked[h][:, t, :], in_=ht[:, t, :].indirect(links))
             else:
-                nc.scalar.activation(out=linked[h, t][:], in_=ht[t][:].indirect(links), func=ACT.Copy)
+                nc.scalar.activation(out=linked[h][:, t, :], in_=ht[:, t, :].indirect(links), func=ACT.Copy)
 
-        p = sbuf("p", [P, SLOTS], F32, tag="ht2")
+        p = sbuf("p", [P, SLOTS], F32, tag="ht")
         z = sbuf("z", [P, 1], F32)
         nc.scalar.activation(out=p[:], in_=scores[:], func=ACT.Exp, bias=neg_max[:], accum_out=z[:])
 
         c0 = psum.tile([P, SLOTS], F32, name="c0")
         for h in range(2):
             cols = slice(HALF * h, HALF * (h + 1))
-            hs1 = sbuf("hs1_%d" % h, [P, PACK, HALF], BF16)
+            hs1 = sbuf("hs1_%d" % h, [P, PACK, HALF], BF16, tag="linked0" if h == 1 else None)
             for t in range(PACK) if h == 0 else (3, 0, 1, 2):
                 nc.vector.scalar_tensor_tensor(
                     out=hs1[:, t, :],
-                    in0=linked[h, t][:],
+                    in0=linked[h][:, t, :],
                     scalar=lam_hsc[:, t : t + 1],
                     in1=own[t][:, cols],
                     op0=ALU.mult,
@@ -201,7 +213,7 @@ def tile_attend_blrlent_soft_kernel(
             hs1_codes, hs1_plane = quantize("hs1_%d" % h, hs1_grouped[:].rearrange("p c j -> p (c j)"), HALF)
             product(c0[:, cols], gout_codes[:], gout_plane[:], hs1_codes[:], hs1_plane[:])
 
-        inv_z = sbuf("inv_z", [P, 1], F32)
+        inv_z = sbuf("inv_z", [P, 1], F32, tag="hs1_grouped1")
         nc.vector.reciprocal(out=inv_z[:], in_=z[:])
         row_factors = sbuf("row_factors", [P, 2], F32)
         nc.vector.tensor_scalar(

@@ -121,11 +121,11 @@ def tile_attend_blrlent_soft_kernel(
         nc.scalar.activation(out=w1_dealt[:, :W1_SCALAR_COLS], in_=w1_source[:, :W1_SCALAR_COLS], func=ACT.Copy)
         nc.vector.tensor_copy(out=w1_dealt[:, W1_SCALAR_COLS:], in_=w1_source[:, W1_SCALAR_COLS:])
         query_rows = load_rows(reused("query_rows", [P, PACK, ROWS], F32, AT_W1 + 2048), query, nc.sync)
-        keys_pool = load_words(reused("keys_pool", [P, POOL], U32, AT_W1 + 4224), keys_words)
-        lam_rows = load_rows(reused("lam_rows", [P, PACK, 1], F32, AT_W1 + 4096), lam, nc.sync)
-        hsc_rows = load_rows(reused("hsc_rows", [P, PACK, 1], F32, AT_W1 + 4160), hsc, nc.sync)
-        keys_bytes = load_scales(reused("keys_bytes", [P, POOL], U8, AT_W1), keys_scales, nc.gpsimd, nc.scalar)
+        lam_rows = load_rows(reused("lam_rows", [P, PACK, 1], F32, AT_W1 + 4096), lam, nc.scalar)
+        hsc_rows = load_rows(reused("hsc_rows", [P, PACK, 1], F32, AT_W1 + 4160), hsc, nc.scalar)
+        keys_bytes = load_scales(reused("keys_bytes", [P, POOL], U8, AT_W1), keys_scales, nc.gpsimd, nc.sync)
         w1_codes, w1_plane = quantize("w1", w1_grouped[:].rearrange("p t m j -> p (t m j)"), HIDDEN)
+        keys_pool = load_words(reused("keys_pool", [P, POOL], U32, AT_GROUPED + 2560), keys_words)
         tab_plane = reused("tab_plane", [P, SLOTS], U8, AT_GROUPED)
         tab_codes = reused("tab_codes", [P, SLOTS], U32, AT_GROUPED + SLOTS)
         for h in range(2):
@@ -137,6 +137,7 @@ def tile_attend_blrlent_soft_kernel(
         old_rows = reused("old_rows", [P, POOL], F32, AT_TAB + 5120)
         nc.sync.dma_start(out=old_rows[:], in_=old)
 
+        query_grouped = interleave_small(sbuf("query_grouped", [P, ROWS, PACK], BF16), query_rows[:])
         zh = {}
         grown = {}
         for h in range(2):
@@ -154,10 +155,9 @@ def tile_attend_blrlent_soft_kernel(
                     out=grown[pair, h][:], in0=grown[pair, h][:], scalar1=EXP_CAP, scalar2=0.0, op0=ALU.min, op1=ALU.max
                 )
 
-        query_grouped = interleave_small(sbuf("query_grouped", [P, ROWS, PACK], BF16), query_rows[:])
-        query_codes, query_plane = quantize("query", query_grouped[:].rearrange("p c j -> p (c j)"), ROWS, AT_TAB + 2304)
-        keys_codes = gather(reused("keys_codes", [P, SLOTS], U32, AT_TAB + 3072), keys_pool, token_list)
-        keys_plane = gather(reused("keys_plane", [P, SLOTS], U8, AT_W1 + 4224), keys_bytes, token_list)
+        keys_plane = gather(reused("keys_plane", [P, SLOTS], U8, AT_TAB + 3072), keys_bytes, token_list)
+        query_codes, query_plane = quantize("query", query_grouped[:].rearrange("p c j -> p (c j)"), ROWS, AT_W1)
+        keys_codes = gather(sbuf("keys_codes", [P, SLOTS], U32), keys_pool, token_list)
         scores = psum.tile([P, SLOTS], F32, name="scores")
         product(scores[:], query_codes[:], query_plane[:], keys_codes[:], keys_plane[:])
         neg_max = sbuf("neg_max", [P, 1], F32)
@@ -176,7 +176,10 @@ def tile_attend_blrlent_soft_kernel(
                     out=ht[:, 2 * pair : 2 * pair + 2, HALF * h : HALF * (h + 1)], in0=logs[:], in1=zh[pair, h][:], op=ALU.max
                 )
         gout_grouped = interleave_small(sbuf("gout_grouped", [P, ROWS, PACK], BF16, tag="grown0_0"), gout_rows[:])
-        gout_codes, gout_plane = quantize("gout", gout_grouped[:].rearrange("p c j -> p (c j)"), ROWS, tag="logs1_1")
+        links = [link_list[:, HALF // 16 * h : HALF // 16 * (h + 1)] for h in range(2)]
+        linked = {}
+        linked[3, 1] = sbuf("linked3_1", [P, HALF], F32)
+        nc.vector.tensor_copy(out=linked[3, 1][:], in_=ht[:, 3, :].indirect(links[1]))
         for t in range(PACK):
             own.append(sbuf("own%d" % t, [P, SLOTS], F32))
             engine = nc.gpsimd if t < 2 else nc.vector
@@ -184,32 +187,41 @@ def tile_attend_blrlent_soft_kernel(
                 out=own[t][:], in0=ht[:, t, :], scalar1=hsc_rows[:, t, :], scalar2=0.0, op0=ALU.mult, op1=ALU.add
             )
 
-        linked = [sbuf("linked%d" % h, [P, PACK, HALF], F32) for h in range(2)]
-        for h, t in [(1, 3)] + [(0, t) for t in range(PACK)] + [(1, 0), (1, 1), (1, 2)]:
-            links = link_list[:, HALF // 16 * h : HALF // 16 * (h + 1)]
-            if h == 1 and t == 3:
-                nc.vector.tensor_copy(out=linked[h][:, t, :], in_=ht[:, t, :].indirect(links))
-            else:
-                nc.scalar.activation(out=linked[h][:, t, :], in_=ht[:, t, :].indirect(links), func=ACT.Copy)
+        ht_row = ht[:].rearrange("p t i -> p (t i)")
+        for t in range(2):
+            linked[t] = sbuf("linked%d" % t, [P, SLOTS], F32)
+            window = ht_row[:, SLOTS * t : SLOTS * (t + 2)]
+            nc.scalar.activation(out=linked[t][:], in_=window.indirect(link_list[:]), func=ACT.Copy)
+        for t, h in ((2, 0), (3, 0), (2, 1)):
+            linked[t, h] = sbuf("linked%d_%d" % (t, h), [P, HALF], F32)
+            nc.scalar.activation(out=linked[t, h][:], in_=ht[:, t, :].indirect(links[h]), func=ACT.Copy)
 
         p = sbuf("p", [P, SLOTS], F32, tag="ht")
         z = sbuf("z", [P, 1], F32)
         nc.scalar.activation(out=p[:], in_=scores[:], func=ACT.Exp, bias=neg_max[:], accum_out=z[:])
 
         c0 = psum.tile([P, SLOTS], F32, name="c0")
+        hs1 = sbuf("hs1", [P, PACK, SLOTS], BF16)
+
+        def combine(t, cols, looked_up):
+            nc.vector.scalar_tensor_tensor(
+                out=hs1[:, t, cols],
+                in0=looked_up[:],
+                scalar=lam_hsc[:, t : t + 1],
+                in1=own[t][:, cols],
+                op0=ALU.mult,
+                op1=ALU.add,
+            )
+
+        for t in range(2):
+            combine(t, slice(0, SLOTS), linked[t])
         for h in range(2):
             cols = slice(HALF * h, HALF * (h + 1))
-            hs1 = sbuf("hs1_%d" % h, [P, PACK, HALF], BF16, tag="linked0" if h == 1 else None)
-            for t in range(PACK) if h == 0 else (3, 0, 1, 2):
-                nc.vector.scalar_tensor_tensor(
-                    out=hs1[:, t, :],
-                    in0=linked[h][:, t, :],
-                    scalar=lam_hsc[:, t : t + 1],
-                    in1=own[t][:, cols],
-                    op0=ALU.mult,
-                    op1=ALU.add,
-                )
-            hs1_grouped = interleave(sbuf("hs1_grouped%d" % h, [P, HALF, PACK], BF16), hs1[:])
+            for t in (2, 3) if h == 0 else (3, 2):
+                combine(t, cols, linked[t, h])
+            if h == 0:
+                gout_codes, gout_plane = quantize("gout", gout_grouped[:].rearrange("p c j -> p (c j)"), ROWS, tag="logs1_1")
+            hs1_grouped = interleave(sbuf("hs1_grouped%d" % h, [P, HALF, PACK], BF16), hs1[:, :, cols])
             hs1_codes, hs1_plane = quantize("hs1_%d" % h, hs1_grouped[:].rearrange("p c j -> p (c j)"), HALF)
             product(c0[:, cols], gout_codes[:], gout_plane[:], hs1_codes[:], hs1_plane[:])
 

@@ -23,7 +23,7 @@ HALF = SLOTS // 2
 GRAD_SCALE = 512.0
 EXP_CAP = 2.0**56
 W1_SCALAR_COLS = 56
-OUT_CHUNKS = (352, 352, 352, 352, 320, 320)
+OUT_CHUNKS = (128, 320, 448, 448, 448, 256)
 
 AT_W1 = 0
 AT_TAB = 12544
@@ -160,8 +160,6 @@ def tile_attend_blrlent_soft_kernel(
         keys_codes = gather(sbuf("keys_codes", [P, SLOTS], U32), keys_pool, token_list)
         scores = psum.tile([P, SLOTS], F32, name="scores")
         product(scores[:], query_codes[:], query_plane[:], keys_codes[:], keys_plane[:])
-        neg_max = sbuf("neg_max", [P, 1], F32)
-        nc.vector.tensor_reduce(out=neg_max[:], in_=scores[:], axis=AXIS_X, op=ALU.max, negate=True)
 
         lam_hsc = sbuf("lam_hsc", [P, PACK], F32)
         nc.vector.tensor_tensor(out=lam_hsc[:], in0=lam_rows[:, :, 0], in1=hsc_rows[:, :, 0], op=ALU.mult)
@@ -178,8 +176,8 @@ def tile_attend_blrlent_soft_kernel(
         gout_grouped = interleave_small(sbuf("gout_grouped", [P, ROWS, PACK], BF16, tag="grown0_0"), gout_rows[:])
         links = [link_list[:, HALF // 16 * h : HALF // 16 * (h + 1)] for h in range(2)]
         linked = {}
-        linked[3, 1] = sbuf("linked3_1", [P, HALF], F32)
-        nc.vector.tensor_copy(out=linked[3, 1][:], in_=ht[:, 3, :].indirect(links[1]))
+        neg_max = sbuf("neg_max", [P, 1], F32, tag="logs1_0")
+        nc.vector.tensor_reduce(out=neg_max[:], in_=scores[:], axis=AXIS_X, op=ALU.max, negate=True)
         for t in range(PACK):
             own.append(sbuf("own%d" % t, [P, SLOTS], F32))
             engine = nc.gpsimd if t < 2 else nc.vector
@@ -192,7 +190,7 @@ def tile_attend_blrlent_soft_kernel(
             linked[t] = sbuf("linked%d" % t, [P, SLOTS], F32)
             window = ht_row[:, SLOTS * t : SLOTS * (t + 2)]
             nc.scalar.activation(out=linked[t][:], in_=window.indirect(link_list[:]), func=ACT.Copy)
-        for t, h in ((2, 0), (3, 0), (2, 1)):
+        for t, h in ((2, 0), (3, 0), (2, 1), (3, 1)):
             linked[t, h] = sbuf("linked%d_%d" % (t, h), [P, HALF], F32)
             nc.scalar.activation(out=linked[t, h][:], in_=ht[:, t, :].indirect(links[h]), func=ACT.Copy)
 
@@ -217,7 +215,7 @@ def tile_attend_blrlent_soft_kernel(
             combine(t, slice(0, SLOTS), linked[t])
         for h in range(2):
             cols = slice(HALF * h, HALF * (h + 1))
-            for t in (2, 3) if h == 0 else (3, 2):
+            for t in (2, 3):
                 combine(t, cols, linked[t, h])
             if h == 0:
                 gout_codes, gout_plane = quantize("gout", gout_grouped[:].rearrange("p c j -> p (c j)"), ROWS, tag="logs1_1")

from contextlib import ExitStack

import concourse.mybir as mybir

F32 = mybir.dt.float32
BF16 = mybir.dt.bfloat16
I32 = mybir.dt.int32
U32 = mybir.dt.uint32
U16 = mybir.dt.uint16
U8 = mybir.dt.uint8
FP8X4 = mybir.dt.float8_e4m3fn_x4
ALU = mybir.AluOpType
ACT = mybir.ActivationFunctionType
AXIS_X = mybir.AxisListType.X

P = 128
PACK = 4
POOL = 2048
SLOTS = 512
HIDDEN = 512
ROWS = 128
HALF = SLOTS // 2
GRAD_SCALE = 512.0
EXP_CAP = 2.0**56
W1_SCALAR_COLS = 56
OUT_CHUNKS = (128, 320, 448, 448, 448, 256)

AT_W1 = 0
AT_TAB = 12544
AT_GROUPED = 25856

FLOPS = 2 * 512 * SLOTS * (ROWS + HIDDEN + ROWS)


def tile_attend_blrlent_soft_kernel(
    tc, query, keys_words, keys_scales, tab_words, tab_scales, w1, lam, gout, hsc, old, offs3, offs, out
):
    nc = tc.nc
    with ExitStack() as ctx:
        held = ctx.enter_context(tc.tile_pool(name="held", bufs=1))
        early = ctx.enter_context(tc.tile_pool(name="early", bufs=1))
        psum = ctx.enter_context(tc.psum_pool(name="psum", bufs=1))

        def sbuf(name, shape, dtype, tag=None):
            return held.tile(shape, dtype, name=name, tag=tag or name, align_bytes=64)

        def reused(name, shape, dtype, offset):
            return early.tile(shape, dtype, name=name, offset=offset, align_bytes=64)

        def load_words(tile, words):
            nc.sync.dma_start(out=tile[:].bitcast(I32), in_=words[0].rearrange("p n t -> p (n t)").bitcast(I32))
            return tile

        def load_scales(tile, scales, clearing, queue):
            clearing.memset(tile[:].bitcast(I32), 0)
            for quad in range(4):
                queue.dma_start(
                    out=tile[32 * quad : 32 * quad + 4, :].bitcast(I32),
                    in_=scales[0, 4 * quad : 4 * quad + 4, :].bitcast(I32),
                )
            return tile

        def load_rows(tile, rows, queue):
            queue.dma_start(out=tile[:], in_=rows.rearrange("(p j) c -> p j c", j=PACK))
            return tile

        def gather(tile, window, offsets):
            nc.vector.tensor_copy(out=tile[:], in_=window[:].indirect(offsets[:]))
            return tile

        def interleave(tile, planes):
            nc.vector.tensor_copy(
                out=tile[:].rearrange("p (c i) j -> p c j i", i=4),
                in_=planes.rearrange("p j (c i) -> p c j i", i=4),
            )
            return tile

        def interleave_small(tile, planes):
            nc.gpsimd.tensor_copy(out=tile[:], in_=planes.rearrange("p j c -> p c j"))
            return tile

        def quantize(name, grouped, width, at=None, tag=None):
            if at is None:
                codes = sbuf(name + "_codes", [P, width], U32, tag)
            else:
                codes = reused(name + "_codes", [P, width], U32, at)
            plane = sbuf(name + "_plane", [P, width], U8)
            nc.vector.quantize_mx(out=codes[:].bitcast(FP8X4), scales=plane[:], in_=grouped)
            return codes, plane

        def product(bank, lhs_codes, lhs_plane, rhs_codes, rhs_plane):
            nc.tensor.matmul_mx(
                out=bank,
                lhsT=lhs_codes.bitcast(FP8X4),
                lhsT_scale=lhs_plane,
                rhs=rhs_codes.bitcast(FP8X4),
                rhs_scale=rhs_plane,
                start=True,
                stop=True,
            )

        token_list = held.tile([P, SLOTS // 16], U16, name="token_list")
        nc.sync.dma_start(token_list[:], offs)
        w1_rows = load_rows(reused("w1_rows", [P, PACK, HIDDEN], F32, AT_W1), w1, nc.sync)
        tab_pool = load_words(reused("tab_pool", [P, POOL], U32, AT_TAB), tab_words)
        tab_bytes = sbuf("tab_bytes", [P, POOL], U8)
        load_scales(tab_bytes, tab_scales, nc.gpsimd, nc.scalar)
        link_list = held.tile([P, SLOTS // 16], U16, name="link_list")
        nc.sync.dma_start(link_list[:], offs3)

        placed = sbuf("placed", [P, POOL], F32)
        nc.gpsimd.memset(placed[:], 0.0)

        constants = sbuf("constants", [P, 2], F32)
        nc.gpsimd.memset(constants[:, 0:1], GRAD_SCALE)
        nc.gpsimd.memset(constants[:, 1:2], -1.0)

        w1_grouped = reused("w1_grouped", [P, PACK, P, PACK], BF16, AT_GROUPED)
        w1_dealt = w1_grouped[:].rearrange("p t m j -> p m t j")
        w1_source = w1_rows[:].rearrange("p j (m t) -> p m t j", t=PACK)
        nc.scalar.activation(out=w1_dealt[:, :W1_SCALAR_COLS], in_=w1_source[:, :W1_SCALAR_COLS], func=ACT.Copy)
        nc.vector.tensor_copy(out=w1_dealt[:, W1_SCALAR_COLS:], in_=w1_source[:, W1_SCALAR_COLS:])
        query_rows = load_rows(reused("query_rows", [P, PACK, ROWS], F32, AT_W1 + 2048), query, nc.sync)
        lam_rows = load_rows(reused("lam_rows", [P, PACK, 1], F32, AT_W1 + 4096), lam, nc.scalar)
        hsc_rows = load_rows(reused("hsc_rows", [P, PACK, 1], F32, AT_W1 + 4160), hsc, nc.scalar)
        keys_bytes = load_scales(reused("keys_bytes", [P, POOL], U8, AT_W1), keys_scales, nc.gpsimd, nc.sync)
        w1_codes, w1_plane = quantize("w1", w1_grouped[:].rearrange("p t m j -> p (t m j)"), HIDDEN)
        keys_pool = load_words(reused("keys_pool", [P, POOL], U32, AT_GROUPED + 2560), keys_words)
        tab_plane = reused("tab_plane", [P, SLOTS], U8, AT_GROUPED)
        tab_codes = reused("tab_codes", [P, SLOTS], U32, AT_GROUPED + SLOTS)
        for h in range(2):
            slots = slice(HALF * h, HALF * (h + 1))
            tokens = token_list[:, HALF // 16 * h : HALF // 16 * (h + 1)]
            nc.vector.tensor_copy(out=tab_plane[:, slots], in_=tab_bytes[:].indirect(tokens))
            nc.vector.tensor_copy(out=tab_codes[:, slots], in_=tab_pool[:].indirect(tokens))
        gout_rows = load_rows(reused("gout_rows", [P, PACK, ROWS], F32, AT_TAB + 128), gout, nc.sync)
        old_rows = reused("old_rows", [P, POOL], F32, AT_TAB + 5120)
        nc.sync.dma_start(out=old_rows[:], in_=old)

        query_grouped = interleave_small(sbuf("query_grouped", [P, ROWS, PACK], BF16), query_rows[:])
        zh = {}
        grown = {}
        for h in range(2):
            slots = slice(HALF * h, HALF * (h + 1))
            for pair in range(2):
                zh[pair, h] = psum.tile([P, 2, HALF], F32, name="zh%d_%d" % (pair, h))
                for e in range(2):
                    cols = slice(P * (2 * pair + e), P * (2 * pair + e + 1))
                    product(
                        zh[pair, h][:, e, :], w1_codes[:, cols], w1_plane[:, cols], tab_codes[:, slots], tab_plane[:, slots]
                    )
                grown[pair, h] = sbuf("grown%d_%d" % (pair, h), [P, 2, HALF], F32)
                nc.scalar.activation(out=grown[pair, h][:], in_=zh[pair, h][:], func=ACT.Exp)
                nc.gpsimd.tensor_scalar(
                    out=grown[pair, h][:], in0=grown[pair, h][:], scalar1=EXP_CAP, scalar2=0.0, op0=ALU.min, op1=ALU.max
                )

        keys_plane = gather(reused("keys_plane", [P, SLOTS], U8, AT_TAB + 3072), keys_bytes, token_list)
        query_codes, query_plane = quantize("query", query_grouped[:].rearrange("p c j -> p (c j)"), ROWS, AT_W1)
        keys_codes = gather(sbuf("keys_codes", [P, SLOTS], U32), keys_pool, token_list)
        scores = psum.tile([P, SLOTS], F32, name="scores")
        product(scores[:], query_codes[:], query_plane[:], keys_codes[:], keys_plane[:])

        lam_hsc = sbuf("lam_hsc", [P, PACK], F32)
        nc.vector.tensor_tensor(out=lam_hsc[:], in0=lam_rows[:, :, 0], in1=hsc_rows[:, :, 0], op=ALU.mult)

        ht = sbuf("ht", [P, PACK, SLOTS], F32)
        own = []
        for pair in range(2):
            for h in range(2):
                logs = sbuf("logs%d_%d" % (pair, h), [P, 2, HALF], F32)
                nc.scalar.activation(out=logs[:], in_=grown[pair, h][:], func=ACT.Ln, bias=1.0)
                nc.vector.tensor_tensor(
                    out=ht[:, 2 * pair : 2 * pair + 2, HALF * h : HALF * (h + 1)], in0=logs[:], in1=zh[pair, h][:], op=ALU.max
                )
        gout_grouped = interleave_small(sbuf("gout_grouped", [P, ROWS, PACK], BF16, tag="grown0_0"), gout_rows[:])
        links = [link_list[:, HALF // 16 * h : HALF // 16 * (h + 1)] for h in range(2)]
        linked = {}
        neg_max = sbuf("neg_max", [P, 1], F32, tag="logs1_0")
        nc.vector.tensor_reduce(out=neg_max[:], in_=scores[:], axis=AXIS_X, op=ALU.max, negate=True)
        for t in range(PACK):
            own.append(sbuf("own%d" % t, [P, SLOTS], F32))
            engine = nc.gpsimd if t < 2 else nc.vector
            engine.tensor_scalar(
                out=own[t][:], in0=ht[:, t, :], scalar1=hsc_rows[:, t, :], scalar2=0.0, op0=ALU.mult, op1=ALU.add
            )

        ht_row = ht[:].rearrange("p t i -> p (t i)")
        for t in range(2):
            linked[t] = sbuf("linked%d" % t, [P, SLOTS], F32)
            window = ht_row[:, SLOTS * t : SLOTS * (t + 2)]
            nc.scalar.activation(out=linked[t][:], in_=window.indirect(link_list[:]), func=ACT.Copy)
        for t, h in ((2, 0), (3, 0), (2, 1), (3, 1)):
            linked[t, h] = sbuf("linked%d_%d" % (t, h), [P, HALF], F32)
            nc.scalar.activation(out=linked[t, h][:], in_=ht[:, t, :].indirect(links[h]), func=ACT.Copy)

        p = sbuf("p", [P, SLOTS], F32, tag="ht")
        z = sbuf("z", [P, 1], F32)
        nc.scalar.activation(out=p[:], in_=scores[:], func=ACT.Exp, bias=neg_max[:], accum_out=z[:])

        c0 = psum.tile([P, SLOTS], F32, name="c0")
        hs1 = sbuf("hs1", [P, PACK, SLOTS], BF16)

        def combine(t, cols, looked_up):
            nc.vector.scalar_tensor_tensor(
                out=hs1[:, t, cols],
                in0=looked_up[:],
                scalar=lam_hsc[:, t : t + 1],
                in1=own[t][:, cols],
                op0=ALU.mult,
                op1=ALU.add,
            )

        for t in range(2):
            combine(t, slice(0, SLOTS), linked[t])
        for h in range(2):
            cols = slice(HALF * h, HALF * (h + 1))
            for t in (2, 3):
                combine(t, cols, linked[t, h])
            if h == 0:
                gout_codes, gout_plane = quantize("gout", gout_grouped[:].rearrange("p c j -> p (c j)"), ROWS, tag="logs1_1")
            hs1_grouped = interleave(sbuf("hs1_grouped%d" % h, [P, HALF, PACK], BF16), hs1[:, :, cols])
            hs1_codes, hs1_plane = quantize("hs1_%d" % h, hs1_grouped[:].rearrange("p c j -> p (c j)"), HALF)
            product(c0[:, cols], gout_codes[:], gout_plane[:], hs1_codes[:], hs1_plane[:])

        inv_z = sbuf("inv_z", [P, 1], F32, tag="hs1_grouped1")
        nc.vector.reciprocal(out=inv_z[:], in_=z[:])
        row_factors = sbuf("row_factors", [P, 2], F32)
        nc.vector.tensor_scalar(
            out=row_factors[:], in0=constants[:], scalar1=inv_z[:], scalar2=None, op0=ALU.mult
        )
        weighted = sbuf("weighted", [P, SLOTS], F32)
        total = sbuf("total", [P, 1], F32)
        nc.vector.scalar_tensor_tensor(
            out=weighted[:], in0=c0[:], scalar=row_factors[:, 0:1], in1=p[:], op0=ALU.mult, op1=ALU.mult, accum_out=total[:]
        )
        through_z = sbuf("through_z", [P, SLOTS], F32)
        nc.vector.tensor_scalar(
            out=through_z[:], in0=p[:], scalar1=total[:], scalar2=row_factors[:, 1:2], op0=ALU.mult, op1=ALU.mult
        )
        nc.vector.tensor_tensor(
            out=placed[:].indirect(token_list[:]), in0=weighted[:], in1=through_z[:], op=ALU.add
        )

        start = 0
        for n, width in enumerate(OUT_CHUNKS):
            cols = slice(start, start + width)
            result = sbuf("result%d" % n, [P, width], F32)
            nc.vector.tensor_tensor(out=result[:], in0=placed[:, cols], in1=old_rows[:, cols], op=ALU.add)
            nc.sync.dma_start(out=out[:, cols], in_=result[:])
            start = start + width
